import numpy as np
import ml_dtypes

BF16 = ml_dtypes.bfloat16


def bf(x):
    return np.asarray(x, np.float32).astype(BF16)


def f32(x):
    return np.asarray(x, np.float32)


def f64(x):
    return np.asarray(x).astype(np.float64)


def striped(idx):
    return np.tile(idx.reshape(-1, 16).T, (8, 1))


S, K, M, N = 4096, 512, 512, 512


def setup_inputs():
    return {"table": bf(np.random.standard_normal((K, S))), "w": bf(np.random.standard_normal((K, M)) / np.sqrt(K)), "b": f32(0.5 * np.random.standard_normal((M, 1))), "offs": striped(np.random.permutation(S)[:N])}


def reference(table, w, b, offs):
    idx = offs[:16].T.reshape(-1)
    x = f64(table)[:, idx]
    y = f64(w).T @ x
    return np.tanh(y + f64(b))

@@ -1,0 +1,48 @@
+import concourse.mybir as mybir
+
+BF16, F32, U16 = mybir.dt.bfloat16, mybir.dt.float32, mybir.dt.uint16
+TANH = mybir.ActivationFunctionType.Tanh
+
+P = 128
+K, S, M, N = 512, 4096, 512, 512
+KB, MB = K // P, M // P
+FLOPS = 2 * K * M * N
+
+
+def tile_gather_matmul_kernel(tc, table, w, b, offs, out):
+    nc = tc.nc
+    with (
+        tc.tile_pool(name="held", bufs=1) as held,
+        tc.tile_pool(name="results", bufs=MB) as results,
+        tc.psum_pool(name="psum", bufs=1) as psum,
+    ):
+        offsets = held.tile([P, N // 16], U16, name="offsets")
+        nc.sync.dma_start(offsets[:], offs)
+
+        weights = held.tile([P, KB, M], BF16, name="weights")
+        nc.sync.dma_start(weights[:], w.rearrange("(a p) m -> p a m", p=P))
+
+        windows = []
+        for kb in range(KB):
+            window = held.tile([P, S], BF16, name=f"window{kb}")
+            nc.sync.dma_start(window[:], table[kb * P : (kb + 1) * P, :])
+            windows.append(window)
+
+        bias = held.tile([P, MB], F32, name="bias")
+        nc.scalar.dma_start(bias[:], b.rearrange("(a p) o -> p (a o)", p=P))
+
+        banks = [psum.tile([P, N], F32, name=f"bank{mb}") for mb in range(MB)]
+        for kb in range(KB):
+            for mb in range(MB):
+                nc.tensor.matmul(
+                    banks[mb][:],
+                    weights[:, kb, mb * P : (mb + 1) * P],
+                    windows[kb][:].indirect(offsets[:]),
+                    start=kb == 0,
+                    stop=kb == KB - 1,
+                )
+
+        for mb in range(MB):
+            result = results.tile([P, N], F32, name="result")
+            nc.scalar.activation(result[:], banks[mb][:], TANH, bias=bias[:, mb : mb + 1])
+            nc.sync.dma_start(out[mb * P : (mb + 1) * P, :], result[:])

@@ -19,13 +19,14 @@ def tile_gather_matmul_kernel(tc, table, w, b, offs, out):
         offsets = held.tile([P, N // 16], U16, name="offsets")
         nc.sync.dma_start(offsets[:], offs)
 
-        weights = held.tile([P, KB, M], BF16, name="weights")
-        nc.sync.dma_start(weights[:], w.rearrange("(a p) m -> p a m", p=P))
-
-        windows = []
+        weights, windows = [], []
         for kb in range(KB):
+            rows = slice(kb * P, (kb + 1) * P)
+            weight = held.tile([P, M], BF16, name=f"weight{kb}")
+            nc.sync.dma_start(weight[:], w[rows, :])
+            weights.append(weight)
             window = held.tile([P, S], BF16, name=f"window{kb}")
-            nc.sync.dma_start(window[:], table[kb * P : (kb + 1) * P, :])
+            nc.sync.dma_start(window[:], table[rows, :])
             windows.append(window)
 
         bias = held.tile([P, MB], F32, name="bias")
@@ -36,7 +37,7 @@ def tile_gather_matmul_kernel(tc, table, w, b, offs, out):
             for mb in range(MB):
                 nc.tensor.matmul(
                     banks[mb][:],
-                    weights[:, kb, mb * P : (mb + 1) * P],
+                    weights[kb][:, mb * P : (mb + 1) * P],
                     windows[kb][:].indirect(offsets[:]),
                     start=kb == 0,
                     stop=kb == KB - 1,

import concourse.mybir as mybir

BF16, F32, U16 = mybir.dt.bfloat16, mybir.dt.float32, mybir.dt.uint16
TANH = mybir.ActivationFunctionType.Tanh

P = 128
K, S, M, N = 512, 4096, 512, 512
KB, MB = K // P, M // P
FLOPS = 2 * K * M * N


def tile_gather_matmul_kernel(tc, table, w, b, offs, out):
    nc = tc.nc
    with (
        tc.tile_pool(name="held", bufs=1) as held,
        tc.tile_pool(name="results", bufs=MB) as results,
        tc.psum_pool(name="psum", bufs=1) as psum,
    ):
        offsets = held.tile([P, N // 16], U16, name="offsets")
        nc.sync.dma_start(offsets[:], offs)

        weights, windows = [], []
        for kb in range(KB):
            rows = slice(kb * P, (kb + 1) * P)
            weight = held.tile([P, M], BF16, name=f"weight{kb}")
            nc.sync.dma_start(weight[:], w[rows, :])
            weights.append(weight)
            window = held.tile([P, S], BF16, name=f"window{kb}")
            nc.sync.dma_start(window[:], table[rows, :])
            windows.append(window)

        bias = held.tile([P, MB], F32, name="bias")
        nc.scalar.dma_start(bias[:], b.rearrange("(a p) o -> p (a o)", p=P))

        banks = [psum.tile([P, N], F32, name=f"bank{mb}") for mb in range(MB)]
        for kb in range(KB):
            for mb in range(MB):
                nc.tensor.matmul(
                    banks[mb][:],
                    weights[kb][:, mb * P : (mb + 1) * P],
                    windows[kb][:].indirect(offsets[:]),
                    start=kb == 0,
                    stop=kb == KB - 1,
                )

        for mb in range(MB):
            result = results.tile([P, N], F32, name="result")
            nc.scalar.activation(result[:], banks[mb][:], TANH, bias=bias[:, mb : mb + 1])
            nc.sync.dma_start(out[mb * P : (mb + 1) * P, :], result[:])
